import numpy as np, ml_dtypes
CORES = [3,7,11,15,131,135,139,143]
N = 8
import mx_ref
BF = ml_dtypes.bfloat16
def entries(a):
    return np.ascontiguousarray(a.T).reshape(-1)
def table(e):
    return np.ascontiguousarray(np.reshape(e, (-1, 16)).T).astype(np.int32)
def cols(t, e):
    v = np.concatenate([t.reshape(128, -1, 4), np.zeros((128, 1, 4), BF)], axis=1)
    return np.ascontiguousarray(v[:, e]).reshape(128, -1)
def f(rng, *shape):
    return mx_ref.flush((rng.standard_normal(shape, dtype=np.float32) * np.exp2(rng.integers(-2, 3, shape[:-1] + (1,)))).astype(BF))
def wide(rng, *shape, cols=0):
    v = rng.standard_normal(shape, dtype=np.float32) * np.exp2(rng.integers(-12, 13, shape)).astype(np.float32)
    if cols: v *= np.repeat(np.exp2(rng.integers(-cols, cols + 1, shape[:-2] + (1, shape[-1] // 4))) * (rng.random(shape[:-2] + (1, shape[-1] // 4)) > 0.0625), 4, axis=-1).astype(np.float32)
    return mx_ref.flush(v.astype(BF))
T, W, UN, CR = 1024, 512, 224, 96
HOST = [0 if k < 128 else 1 for k in CORES]
def lists(rng, full=False, alike=False):
    uni, need, pos = np.full((N, 2, UN), -1), np.full((N, N, CR), -1), []
    for q in range(N):
        for g in range(2):
            mates = [r for r in range(N) if HOST[r] == g]
            n = UN if full else int(rng.integers(CR >> 1, CR + 1)) if alike else int(rng.integers(UN >> 2, UN + 1))
            at = rng.permutation(UN)[:n]
            uni[q, g, at] = rng.permutation(T)[:n]
            who = rng.permutation(np.repeat(np.arange(len(mates)), CR))[:n]
            for i, r in enumerate(mates):
                e, others = at[who == i], at[who != i]
                if alike: e = at
                else:
                    k = CR if full else int(rng.integers(max(len(e), CR >> 2), min(CR, n) + 1))
                    e = np.concatenate([e, rng.permutation(others)[:k - len(e)]])
                need[r, q, rng.permutation(CR)[:len(e)]] = e
    for r in range(N):
        ok = np.flatnonzero(need[r].reshape(-1) >= 0)
        pos.append(table(rng.permutation(ok)[:W] if full else rng.choice(ok, W)))
    return {"uni": np.stack([table(e.reshape(-1)) for e in uni]), "need": np.stack([table(e.reshape(-1)) for e in need]), "pos": np.stack(pos)}
def setup_inputs(rng):
    return {"c": f(rng, N, 128, 4 * T), "w": f(rng, N, 128, 512), **lists(rng)}
def setup_inputs_alike(rng):
    return {**setup_inputs(rng), **lists(rng, alike=True)}
def setup_inputs_pairs(rng):
    d = setup_inputs(rng)
    uni, need = np.full((N, 2, UN), -1), np.full((N, N, CR), -1)
    for g in range(2):
        mates = rng.permutation([r for r in range(N) if HOST[r] == g])
        for q in range(N):
            at = rng.permutation(UN)[:2 * CR]
            uni[q, g, at] = rng.permutation(T)[:2 * CR]
            for i, r in enumerate(mates):
                need[r, q] = rng.permutation(at[:CR] if i < len(mates) // 2 else at[CR:])
    pos = [table(rng.choice(N * CR, W)) for r in range(N)]
    return {**d, "uni": np.stack([table(e.reshape(-1)) for e in uni]), "need": np.stack([table(e.reshape(-1)) for e in need]), "pos": np.stack(pos)}
def setup_inputs_full(rng):
    return {**setup_inputs(rng), **lists(rng, full=True)}
def setup_inputs_few(rng):
    d = {**setup_inputs(rng), **lists(rng, full=True)}
    uni = np.stack([entries(e) for e in d["uni"]]).reshape(N, 2, UN)
    need = np.stack([entries(e) for e in d["need"]]).reshape(N, N, CR)
    pos = [None] * N
    for g in range(2):
        p = rng.permutation(N)
        h = [HOST[q] for q in p]
        lead = [h.index(0), h.index(1)]
        own = np.concatenate([p[lead], np.delete(p, lead)])[:-(-W // CR)]
        rest = np.setdiff1d(np.arange(N), own)
        uni[rest, g] = -1
        for r in range(N):
            if HOST[r] != g: continue
            need[r, rest] = -1
            s = rng.permutation(own)[:, None] * CR + np.arange(CR)
            s[-1] = rng.permutation(s[-1])
            pos[r] = table(rng.permutation(s.reshape(-1)[:W]))
    return {**d, "uni": np.stack([table(e.reshape(-1)) for e in uni]), "need": np.stack([table(e.reshape(-1)) for e in need]), "pos": np.stack(pos)}
def setup_inputs_spread(rng):
    d = setup_inputs(rng); d["c"] = wide(rng, N, 128, 4 * T, cols=6); return d
def check_inputs(d):
    b = []
    uni = np.stack([entries(e) for e in d["uni"]]).reshape(N, 2, UN)
    need = np.stack([entries(e) for e in d["need"]]).reshape(N, N, CR)
    if uni.min() < -1 or uni.max() >= T: b.append("uni")
    if need.min() < -1 or need.max() >= UN: return b + ["need"]
    for q in range(N):
        for g in range(2):
            e = uni[q, g][uni[q, g] >= 0]
            if len(set(e.tolist())) != len(e): b.append("a column of one owner twice for one host")
            named = set()
            for r in range(N):
                if HOST[r] != g: continue
                k = need[r, q][need[r, q] >= 0]
                if len(set(k.tolist())) != len(k): b.append("need names an entry of one union twice")
                if (uni[q, g][k] < 0).any(): b.append("need names an empty entry of uni")
                named |= set(k.tolist())
            if set(np.flatnonzero(uni[q, g] >= 0).tolist()) - named: b.append("an entry of uni that no rank of the host needs")
    for r in range(N):
        p = entries(d["pos"][r])
        if p.min() < 0 or p.max() >= N * CR or (need[r].reshape(-1)[p] < 0).any(): b.append("pos")
    return b
def reference(c, w, uni, need, pos):
    uni = np.stack([entries(e) for e in uni]).reshape(N, 2, UN)
    need = np.stack([entries(e) for e in need]).reshape(N, N, CR)
    y = np.zeros((N, 128, W), np.float32)
    for r in range(N):
        g = HOST[r]
        t = np.concatenate([cols(c[q], np.where(need[r, q] >= 0, uni[q, g][need[r, q]], -1)) for q in range(N)], axis=1)
        y[r] = mx_ref.matmul(mx_ref.quantize(w[r]), mx_ref.quantize(cols(t, entries(pos[r]))))
    return {"y": y}

@@ -1,0 +1,253 @@
+from concourse.bass import DstId, RemoteDMATransfer
+from concourse.mybir import dt, ActivationFunctionType
+
+TC, W, UN, CR = 1024, 512, 224, 96
+N = 8
+UC, CC = UN // 16, CR // 16
+C1, C2 = 512, 896
+LW = (N // 2 + 1) * CC
+MIN = 128
+CODES, PLANE = "float8_e4m3fn_x4", "uint8"
+
+SCRATCH = {
+    "needi": ("sbuf", [128, N * CC], "int32"),
+    "unii": ("sbuf", [128, 2 * UC], "int32"),
+    "posi": ("sbuf", [128, W // 16], "int32"),
+    "noff": ("sbuf", [128, N * CC], "uint16"),
+    "nland": ("sbuf", [128, 3 * LW], "uint16"),
+    "uoff": ("sbuf", [128, 2 * UC], "uint16"),
+    "poff": ("sbuf", [128, W // 16], "uint16"),
+    "ct": ("sbuf", [128, 4 * TC], "bfloat16"),
+    "wt": ("sbuf", [128, 512], "bfloat16"),
+    "qc": ("sbuf", [128, TC], CODES), "sc": ("sbuf", [128, TC], PLANE),
+    "qw": ("sbuf", [128, 128], CODES), "sw": ("sbuf", [128, 128], PLANE),
+    "qru": ("sbuf", [128, UN], CODES), "sru": ("sbuf", [128, UN], PLANE),
+    "qou": ("sbuf", [128, UN], CODES), "sou": ("sbuf", [128, UN], PLANE),
+    "qgu": ("sbuf", [128, UN], CODES), "sgu": ("sbuf", [128, UN], PLANE),
+    "qop": ("sbuf", [128, 3 * CR], CODES), "sop": ("sbuf", [128, 3 * CR], PLANE),
+    "qgp": ("sbuf", [128, 3 * CR], CODES), "sgp": ("sbuf", [128, 3 * CR], PLANE),
+    "qb": ("sbuf", [128, N * CR], CODES), "sb": ("sbuf", [128, N * CR], PLANE),
+    "res": ("sbuf", [128, N * CR], "float32"),
+    "yt": ("sbuf", [128, W], "float32"),
+    "ps": ("psum", [128, 5 * 512], "float32"),
+}
+SEMAPHORES = ["d_need", "d_uni", "d_c1", "d_c2", "d_c3", "d_w", "d_pos", "d_y",
+              "v_no", "v_uo", "v_q", "v_qw", "v_po", "v_ru", "v_ou", "v_op", "v_gp", "v_b", "v_c", "v_y",
+              "a_ru", "a_ou", "a_op", "a_gp", "a_b", "a_c", "a_y",
+              "t_0", "t_1", "t_2", "t_3", "t_4",
+              "r_list", "r_uq", "r_us", "r_oq", "r_os",
+              "r_gq0", "r_gq1", "r_gq2", "r_gs0", "r_gs1", "r_gs2", "ls"]
+
+
+def rank_program(g, core, T, topo):
+    if T.rank_of(core) is None:
+        return
+    S = T.sem
+    COPY = ActivationFunctionType.Copy
+    cores = list(T.cores)
+    rank_of = {c: r for r, c in enumerate(cores)}
+
+    def home(c):
+        return [d for d in cores if topo.host(d) == topo.host(c)]
+
+    def mates_of(c):
+        on = topo.cores_of(c)
+        m = [d for d in home(c) if d != c]
+        return [d for d in m if d in on] + [d for d in m if d not in on]
+
+    def place(m, c):
+        return mates_of(m).index(c)
+
+    def partner(c):
+        return [d for d in cores if topo.host(d) != topo.host(c) and topo.same_plane(c, d) and topo.die(d) == topo.die(c)][0]
+
+    mates, mine = mates_of(core), home(core)
+    par = partner(core)
+    h = topo.host(core) - topo.host(cores[0])
+    oh = 1 - h
+
+    def bits(es):
+        return sum(1 << e for e in es)
+
+    def engines(c, m, whole):
+        ms = mates_of(c)
+        leave = topo.engines(c, ms[1])
+        if m == ms[0]:
+            return [e for e in topo.engines(c, m) if e not in leave]
+        if whole:
+            return leave
+        n = len(leave) // 2
+        return leave[:n] if m == ms[1] else leave[n:]
+
+    sent = []
+
+    def to_mates(js, src, dst, sem, whole):
+        tr = []
+        for j in js:
+            m = mates[j]
+            rid, pid = topo.addr(m, core)
+            es = engines(core, m, whole)
+            sent.append(len(es))
+            tr.append(RemoteDMATransfer(dst_ids=[DstId(rid=rid, pnc=pid)], dma_engine_mask=bits(es), remote_sem=sem(m),
+                                        src=src(j), dst=dst(m)))
+        g.remote_dma_fused(tr, local_sem=S.ls)
+
+    def n_from(m, whole):
+        return len(engines(m, core, whole))
+
+    def n_in(whole):
+        return sum(n_from(m, whole) for m in mates)
+    par_eng = topo.engines(core, par)
+    n_par_in = len(topo.engines(par, core))
+
+    def load_list(queue, ks, out, in_, sem):
+        for k in ks:
+            queue.dma_start(out[16 * k:16 * k + 16, :], in_[:, :]).then_inc(sem, 16)
+    V, A = g.vector, g.scalar
+    g.sync.dma_start(T.ct[:, 0:4 * C1], T.c[:, 0:4 * C1]).then_inc(S.d_c1, 16)
+    load_list(g.sync, range(4), T.needi, T.need, S.d_need)
+    load_list(g.sync, range(4), T.unii, T.uni, S.d_uni)
+    g.sync.dma_start(T.ct[:, 4 * C1:4 * C2], T.c[:, 4 * C1:4 * C2]).then_inc(S.d_c2, 16)
+    g.sync.dma_start(T.ct[:, 4 * C2:4 * TC], T.c[:, 4 * C2:4 * TC]).then_inc(S.d_c3, 16)
+    g.sync.dma_start(T.wt[:, :], T.w[:, :]).then_inc(S.d_w, 16)
+    load_list(g.sync, range(8), T.posi, T.pos, S.d_pos)
+    load_list(A, range(4, 8), T.needi, T.need, S.d_need)
+    load_list(A, range(4, 8), T.unii, T.uni, S.d_uni)
+
+    V.wait_ge(S.d_need, 128)
+    V.tensor_copy(T.noff[:, :], T.needi[:, :]).then_inc(S.v_no, 1)
+
+    def quant(a, b, sem):
+        V.wait_ge(sem, 16)
+        V.quantize_mx(T.qc[:, a:b], T.sc[:, a:b], T.ct[:, 4 * a:4 * b]).then_inc(S.v_q, 1)
+    quant(0, C1, S.d_c1)
+    quant(C1, C2, S.d_c2)
+    V.wait_ge(S.d_uni, 128)
+    V.tensor_copy(T.uoff[:, :], T.unii[:, :]).then_inc(S.v_uo, 1)
+    quant(C2, TC, S.d_c3)
+
+    def pick_q(out, a, n, win, offs, sem):
+        V.tensor_copy(out[:, a:a + n].bitcast(dt.uint32), win[:, :].bitcast(dt.uint32).indirect(offs)).then_inc(sem, 1)
+
+    def pick_s(out, a, n, win, offs, sem):
+        A.activation(out[:, a:a + n], win[:, :].indirect(offs), COPY).then_inc(sem, 1)
+
+    def wanted(j, c):
+        a = j * LW + (rank_of[c] - min(rank_of[core], rank_of[par])) * CC
+        return T.nland[:, a:a + CC]
+
+    def own_need(c):
+        return T.noff[:, rank_of[c] * CC:(rank_of[c] + 1) * CC]
+    slot = mine.index(core)
+    uo_far, uo_near = T.uoff[:, oh * UC:(oh + 1) * UC], T.uoff[:, h * UC:(h + 1) * UC]
+    OP = {2: 0, 1: CR, 0: 2 * CR}
+    GP = {1: 0, 0: CR, 2: 2 * CR}
+
+    V.wait_ge(S.v_uo, 1)
+    V.wait_ge(S.v_q, 3)
+    pick_q(T.qru, 0, UN, T.qc, uo_far, S.v_ru)
+    pick_q(T.qou, 0, UN, T.qc, uo_near, S.v_ou)
+    V.wait_ge(S.v_ou, 1)
+    V.wait_ge(S.r_list, n_in(False))
+    for j in OP:
+        pick_q(T.qop, OP[j], CR, T.qou, wanted(j, core), S.v_op)
+    V.wait_ge(S.v_no, 1)
+    pick_q(T.qb, slot * CR, CR, T.qou, own_need(core), S.v_b)
+    V.wait_ge(S.d_w, 16)
+    V.quantize_mx(T.qw[:, 0:128], T.sw[:, 0:128], T.wt[:, 0:512]).then_inc(S.v_qw, 1)
+    A.wait_ge(S.v_uo, 1)
+    A.wait_ge(S.v_q, 3)
+    pick_s(T.sru, 0, UN, T.sc, uo_far, S.a_ru)
+    pick_s(T.sou, 0, UN, T.sc, uo_near, S.a_ou)
+    A.wait_ge(S.a_ou, 1)
+    A.wait_ge(S.r_list, n_in(False))
+    for j in OP:
+        pick_s(T.sop, OP[j], CR, T.sou, wanted(j, core), S.a_op)
+    A.wait_ge(S.v_no, 1)
+    pick_s(T.sb, slot * CR, CR, T.sou, own_need(core), S.a_b)
+    V.wait_ge(S.r_uq, n_par_in)
+    for j in GP:
+        pick_q(T.qgp, GP[j], CR, T.qgu, wanted(j, par), S.v_gp)
+    pick_q(T.qb, 4 * CR, CR, T.qgu, own_need(par), S.v_b)
+    V.wait_ge(S.d_pos, 128)
+    V.tensor_copy(T.poff[:, :], T.posi[:, :]).then_inc(S.v_po, 1)
+    A.wait_ge(S.r_us, n_par_in)
+    for j in GP:
+        pick_s(T.sgp, GP[j], CR, T.sgu, wanted(j, par), S.a_gp)
+    pick_s(T.sb, 4 * CR, CR, T.sgu, own_need(par), S.a_b)
+
+    t = g.tensor
+
+    def product(k, a, b):
+        t.matmul_mx(T.ps[:, 512 * k:512 * k + b - a], T.qw[:, 0:128], T.sw[:, 0:128], T.qb[:, a:b], T.sb[:, a:b],
+                    True, True).then_inc(S["t_%d" % k], 1)
+    t.wait_ge(S.v_qw, 1)
+    t.wait_ge(S.v_b, 2)
+    t.wait_ge(S.a_b, 2)
+    t.wait_ge(S.r_oq, n_in(True))
+    t.wait_ge(S.r_os, n_in(False))
+    product(0, 0, 4 * CR)
+    product(1, 5 * CR - MIN, 5 * CR)
+    for j, m in enumerate(mates):
+        t.wait_ge(S["r_gq%d" % j], n_from(m, True))
+        t.wait_ge(S["r_gs%d" % j], n_from(m, False))
+        product(2 + j, (6 + j) * CR - MIN, (6 + j) * CR)
+
+    def new(k):
+        return T.ps[:, 512 * k + MIN - CR:512 * k + MIN]
+
+    def res_of(c):
+        q = rank_of[c]
+        return T.res[:, q * CR:(q + 1) * CR]
+    lo = rank_of[mine[0]] * CR
+    A.wait_ge(S.t_0, 1)
+    A.activation(T.res[:, lo:lo + 4 * CR], T.ps[:, 0:4 * CR], COPY).then_inc(S.a_c, 1)
+    A.wait_ge(S.t_4, 1)
+    A.activation(res_of(partner(mates[2])), new(4), COPY).then_inc(S.a_c, 1)
+    for k, c in ((1, par), (2, partner(mates[0])), (3, partner(mates[1]))):
+        V.wait_ge(S["t_%d" % k], 1)
+        V.tensor_copy(res_of(c), new(k)).then_inc(S.v_c, 1)
+    for q in (V, A):
+        q.wait_ge(S.v_po, 1)
+        q.wait_ge(S.v_c, 3)
+        q.wait_ge(S.a_c, 2)
+    V.tensor_copy(T.yt[:, 0:W // 2], T.res[:, :].indirect(T.poff[:, 0:16])).then_inc(S.v_y, 1)
+    A.activation(T.yt[:, W // 2:W], T.res[:, :].indirect(T.poff[:, 16:32]), COPY).then_inc(S.a_y, 1)
+    g.sync.wait_ge(S.v_y, 1)
+    g.sync.wait_ge(S.a_y, 1)
+    g.sync.dma_start(T.y[:, :], T.yt[:, :]).then_inc(S.d_y, 16)
+    g.sync.wait_ge(S.d_y, 16)
+
+    def span(m):
+        a = min(rank_of[m], rank_of[partner(m)]) * CC
+        return T.noff[:, a:a + LW]
+
+    def q8(t, a, n):
+        return t[:, a:a + n].bitcast(dt.uint8)
+
+    def s8(t, a, n):
+        return t[:, a:a + n]
+    g.wait_ge(S.v_no, 1)
+    to_mates((0, 1, 2), lambda j: span(mates[j]), lambda m: T.nland[:, place(m, core) * LW:(place(m, core) + 1) * LW],
+             lambda m: S.r_list, False)
+    rid, pid = topo.addr(par, core)
+    for picked, view, dst, src, arrived in ((S.v_ru, q8, T.qgu, T.qru, S.r_uq), (S.a_ru, s8, T.sgu, T.sru, S.r_us)):
+        g.wait_ge(picked, 1)
+        g.remote_dma(out_ap=view(dst, 0, UN), in_ap=view(src, 0, UN), remote_sem=arrived, local_sem=S.ls, pid=pid,
+                     routing_id=rid, dma_engine_mask=bits(par_eng))
+    for k, js in ((1, (2,)), (3, (1, 0))):
+        g.wait_ge(S.v_op, k)
+        to_mates(js, lambda j: q8(T.qop, OP[j], CR), lambda m: q8(T.qb, slot * CR, CR), lambda m: S.r_oq, True)
+    g.wait_ge(S.a_op, 3)
+    to_mates((0, 1, 2), lambda j: s8(T.sop, OP[j], CR), lambda m: s8(T.sb, slot * CR, CR), lambda m: S.r_os, False)
+
+    def at(m):
+        return (5 + place(m, core)) * CR
+    for k, js in ((1, (1,)), (3, (0, 2))):
+        g.wait_ge(S.v_gp, k)
+        to_mates(js, lambda j: q8(T.qgp, GP[j], CR), lambda m: q8(T.qb, at(m), CR),
+                 lambda m: S["r_gq%d" % place(m, core)], True)
+    g.wait_ge(S.a_gp, 3)
+    to_mates((0, 1, 2), lambda j: s8(T.sgp, GP[j], CR), lambda m: s8(T.sb, at(m), CR),
+             lambda m: S["r_gs%d" % place(m, core)], False)
+    g.wait_ge(S.ls, 2 * len(par_eng) + sum(sent))

@@ -4,19 +4,19 @@ from concourse.mybir import dt, ActivationFunctionType
 TC, W, UN, CR = 1024, 512, 224, 96
 N = 8
 UC, CC = UN // 16, CR // 16
-C1, C2 = 512, 896
+CUTS = (0, 192, 640, 896, TC)
+U1 = 64
 LW = (N // 2 + 1) * CC
+U0, P0 = N * CC, N * CC + 2 * UC
+NU = P0 + W // 16
 MIN = 128
+YCUTS = (0, 64, 160, W // 2)
 CODES, PLANE = "float8_e4m3fn_x4", "uint8"
 
 SCRATCH = {
-    "needi": ("sbuf", [128, N * CC], "int32"),
-    "unii": ("sbuf", [128, 2 * UC], "int32"),
-    "posi": ("sbuf", [128, W // 16], "int32"),
-    "noff": ("sbuf", [128, N * CC], "uint16"),
+    "lsti": ("sbuf", [128, NU], "int32"),
+    "loff": ("sbuf", [128, NU], "uint16"),
     "nland": ("sbuf", [128, 3 * LW], "uint16"),
-    "uoff": ("sbuf", [128, 2 * UC], "uint16"),
-    "poff": ("sbuf", [128, W // 16], "uint16"),
     "ct": ("sbuf", [128, 4 * TC], "bfloat16"),
     "wt": ("sbuf", [128, 512], "bfloat16"),
     "qc": ("sbuf", [128, TC], CODES), "sc": ("sbuf", [128, TC], PLANE),
@@ -24,19 +24,18 @@ SCRATCH = {
     "qru": ("sbuf", [128, UN], CODES), "sru": ("sbuf", [128, UN], PLANE),
     "qou": ("sbuf", [128, UN], CODES), "sou": ("sbuf", [128, UN], PLANE),
     "qgu": ("sbuf", [128, UN], CODES), "sgu": ("sbuf", [128, UN], PLANE),
-    "qop": ("sbuf", [128, 3 * CR], CODES), "sop": ("sbuf", [128, 3 * CR], PLANE),
-    "qgp": ("sbuf", [128, 3 * CR], CODES), "sgp": ("sbuf", [128, 3 * CR], PLANE),
+    "qp": ("sbuf", [128, 6 * CR], CODES), "sp": ("sbuf", [128, 6 * CR], PLANE),
     "qb": ("sbuf", [128, N * CR], CODES), "sb": ("sbuf", [128, N * CR], PLANE),
     "res": ("sbuf", [128, N * CR], "float32"),
     "yt": ("sbuf", [128, W], "float32"),
     "ps": ("psum", [128, 5 * 512], "float32"),
 }
-SEMAPHORES = ["d_need", "d_uni", "d_c1", "d_c2", "d_c3", "d_w", "d_pos", "d_y",
-              "v_no", "v_uo", "v_q", "v_qw", "v_po", "v_ru", "v_ou", "v_op", "v_gp", "v_b", "v_c", "v_y",
-              "a_ru", "a_ou", "a_op", "a_gp", "a_b", "a_c", "a_y",
+SEMAPHORES = ["d_lst", "d_c0", "d_c1", "d_c2", "d_c3", "d_w", "d_y",
+              "v_lo", "v_q", "v_qw", "v_ru", "v_ou", "v_op", "v_gp", "v_b", "v_c", "v_y",
+              "a_ru", "a_ou", "a_p", "a_b", "a_c", "a_y",
               "t_0", "t_1", "t_2", "t_3", "t_4",
-              "r_list", "r_uq", "r_us", "r_oq", "r_os",
-              "r_gq0", "r_gq1", "r_gq2", "r_gs0", "r_gs1", "r_gs2", "ls"]
+              "r_list", "r_uq", "r_us", "r_oq", "r_s",
+              "r_gq0", "r_gq1", "r_gq2", "ls"]
 
 
 def rank_program(g, core, T, topo):
@@ -53,7 +52,9 @@ def rank_program(g, core, T, topo):
     def mates_of(c):
         on = topo.cores_of(c)
         m = [d for d in home(c) if d != c]
-        return [d for d in m if d in on] + [d for d in m if d not in on]
+        off = [d for d in m if d not in on]
+        return ([d for d in m if d in on] + [d for d in off if topo.die(d) != topo.die(c)]
+                + [d for d in off if topo.die(d) == topo.die(c)])
 
     def place(m, c):
         return mates_of(m).index(c)
@@ -61,7 +62,7 @@ def rank_program(g, core, T, topo):
     def partner(c):
         return [d for d in cores if topo.host(d) != topo.host(c) and topo.same_plane(c, d) and topo.die(d) == topo.die(c)][0]
 
-    mates, mine = mates_of(core), home(core)
+    mates = mates_of(core)
     par = partner(core)
     h = topo.host(core) - topo.host(cores[0])
     oh = 1 - h
@@ -100,31 +101,26 @@ def rank_program(g, core, T, topo):
     par_eng = topo.engines(core, par)
     n_par_in = len(topo.engines(par, core))
 
-    def load_list(queue, ks, out, in_, sem):
-        for k in ks:
-            queue.dma_start(out[16 * k:16 * k + 16, :], in_[:, :]).then_inc(sem, 16)
     V, A = g.vector, g.scalar
-    g.sync.dma_start(T.ct[:, 0:4 * C1], T.c[:, 0:4 * C1]).then_inc(S.d_c1, 16)
-    load_list(g.sync, range(4), T.needi, T.need, S.d_need)
-    load_list(g.sync, range(4), T.unii, T.uni, S.d_uni)
-    g.sync.dma_start(T.ct[:, 4 * C1:4 * C2], T.c[:, 4 * C1:4 * C2]).then_inc(S.d_c2, 16)
-    g.sync.dma_start(T.ct[:, 4 * C2:4 * TC], T.c[:, 4 * C2:4 * TC]).then_inc(S.d_c3, 16)
+
+    def load_c(k):
+        a, b = CUTS[k], CUTS[k + 1]
+        g.sync.dma_start(T.ct[:, 4 * a:4 * b], T.c[:, 4 * a:4 * b]).then_inc(S["d_c%d" % k], 16)
+    load_c(0)
+    for k, queue in enumerate((g.sync, A)):
+        for a, b, lst in ((0, U0, T.need), (U0, P0, T.uni), (P0, NU, T.pos)):
+            queue.dma_start(T.lsti[16 * k:16 * k + 16, a:b], lst[:, :]).then_inc(S.d_lst, 16)
+    for k in range(1, 4):
+        load_c(k)
     g.sync.dma_start(T.wt[:, :], T.w[:, :]).then_inc(S.d_w, 16)
-    load_list(g.sync, range(8), T.posi, T.pos, S.d_pos)
-    load_list(A, range(4, 8), T.needi, T.need, S.d_need)
-    load_list(A, range(4, 8), T.unii, T.uni, S.d_uni)
 
-    V.wait_ge(S.d_need, 128)
-    V.tensor_copy(T.noff[:, :], T.needi[:, :]).then_inc(S.v_no, 1)
-
-    def quant(a, b, sem):
-        V.wait_ge(sem, 16)
+    V.wait_ge(S.d_lst, 96)
+    for k in range(4):
+        V.tensor_copy(T.loff[32 * k:32 * k + 32, :], T.lsti[0:32, :]).then_inc(S.v_lo, 1)
+    for k in range(4):
+        a, b = CUTS[k], CUTS[k + 1]
+        V.wait_ge(S["d_c%d" % k], 16)
         V.quantize_mx(T.qc[:, a:b], T.sc[:, a:b], T.ct[:, 4 * a:4 * b]).then_inc(S.v_q, 1)
-    quant(0, C1, S.d_c1)
-    quant(C1, C2, S.d_c2)
-    V.wait_ge(S.d_uni, 128)
-    V.tensor_copy(T.uoff[:, :], T.unii[:, :]).then_inc(S.v_uo, 1)
-    quant(C2, TC, S.d_c3)
 
     def pick_q(out, a, n, win, offs, sem):
         V.tensor_copy(out[:, a:a + n].bitcast(dt.uint32), win[:, :].bitcast(dt.uint32).indirect(offs)).then_inc(sem, 1)
@@ -137,117 +133,129 @@ def rank_program(g, core, T, topo):
         return T.nland[:, a:a + CC]
 
     def own_need(c):
-        return T.noff[:, rank_of[c] * CC:(rank_of[c] + 1) * CC]
-    slot = mine.index(core)
-    uo_far, uo_near = T.uoff[:, oh * UC:(oh + 1) * UC], T.uoff[:, h * UC:(h + 1) * UC]
-    OP = {2: 0, 1: CR, 0: 2 * CR}
-    GP = {1: 0, 0: CR, 2: 2 * CR}
+        return T.loff[:, rank_of[c] * CC:(rank_of[c] + 1) * CC]
 
-    V.wait_ge(S.v_uo, 1)
-    V.wait_ge(S.v_q, 3)
-    pick_q(T.qru, 0, UN, T.qc, uo_far, S.v_ru)
-    pick_q(T.qou, 0, UN, T.qc, uo_near, S.v_ou)
-    V.wait_ge(S.v_ou, 1)
-    V.wait_ge(S.r_list, n_in(False))
-    for j in OP:
-        pick_q(T.qop, OP[j], CR, T.qou, wanted(j, core), S.v_op)
-    V.wait_ge(S.v_no, 1)
-    pick_q(T.qb, slot * CR, CR, T.qou, own_need(core), S.v_b)
+    def uni(hh, a, b):
+        return T.loff[:, U0 + hh * UC + a // 16:U0 + hh * UC + b // 16]
+    GP = (1, 0, 2)
+    PARTS = [(None, True), (None, False), (1, False), (1, True), (0, True), (0, False), (2, False), (2, True)]
+
+    def at(j, far):
+        return PARTS.index((j, far)) * CR
+
+    def pair(j):
+        return min(at(j, False), at(j, True))
+
+    def out_at(j, far):
+        return 2 * j * CR + at(j, far) - pair(j)
+
+    for q, pick, far, near, win, out, s_ru, s_ou, s_op in (
+            (V, pick_q, T.qru, T.qou, T.qc, T.qp, S.v_ru, S.v_ou, S.v_op),
+            (A, pick_s, T.sru, T.sou, T.sc, T.sp, S.a_ru, S.a_ou, S.a_p)):
+        q.wait_ge(S.v_lo, 4)
+        q.wait_ge(S.v_q, 4)
+        for a, b in ((0, U1), (U1, UN)):
+            pick(far, a, b - a, win, uni(oh, a, b), s_ru)
+        pick(near, 0, UN, win, uni(h, 0, UN), s_ou)
+        q.wait_ge(s_ou, 1)
+        q.wait_ge(S.r_list, n_in(False))
+        for j in range(3):
+            pick(out, out_at(j, False), CR, near, wanted(j, core), s_op)
+    pick_q(T.qb, at(None, False), CR, T.qou, own_need(core), S.v_b)
     V.wait_ge(S.d_w, 16)
     V.quantize_mx(T.qw[:, 0:128], T.sw[:, 0:128], T.wt[:, 0:512]).then_inc(S.v_qw, 1)
-    A.wait_ge(S.v_uo, 1)
-    A.wait_ge(S.v_q, 3)
-    pick_s(T.sru, 0, UN, T.sc, uo_far, S.a_ru)
-    pick_s(T.sou, 0, UN, T.sc, uo_near, S.a_ou)
-    A.wait_ge(S.a_ou, 1)
-    A.wait_ge(S.r_list, n_in(False))
-    for j in OP:
-        pick_s(T.sop, OP[j], CR, T.sou, wanted(j, core), S.a_op)
-    A.wait_ge(S.v_no, 1)
-    pick_s(T.sb, slot * CR, CR, T.sou, own_need(core), S.a_b)
-    V.wait_ge(S.r_uq, n_par_in)
+    V.wait_ge(S.r_uq, 2 * n_par_in)
     for j in GP:
-        pick_q(T.qgp, GP[j], CR, T.qgu, wanted(j, par), S.v_gp)
-    pick_q(T.qb, 4 * CR, CR, T.qgu, own_need(par), S.v_b)
-    V.wait_ge(S.d_pos, 128)
-    V.tensor_copy(T.poff[:, :], T.posi[:, :]).then_inc(S.v_po, 1)
+        pick_q(T.qp, out_at(j, True), CR, T.qgu, wanted(j, par), S.v_gp)
+    pick_q(T.qb, at(None, True), CR, T.qgu, own_need(par), S.v_b)
     A.wait_ge(S.r_us, n_par_in)
     for j in GP:
-        pick_s(T.sgp, GP[j], CR, T.sgu, wanted(j, par), S.a_gp)
-    pick_s(T.sb, 4 * CR, CR, T.sgu, own_need(par), S.a_b)
+        pick_s(T.sp, out_at(j, True), CR, T.sgu, wanted(j, par), S.a_p)
+    pick_s(T.sb, at(None, False), CR, T.sou, own_need(core), S.a_b)
+    pick_s(T.sb, at(None, True), CR, T.sgu, own_need(par), S.a_b)
 
     t = g.tensor
+    BANKS = [(at(0, False), at(2, True), PARTS[5:7]), (0, at(1, True), PARTS[0:3]),
+             (at(0, True) - MIN, at(0, True), PARTS[3:4]), (at(0, True), at(0, True) + MIN, PARTS[4:5]),
+             (N * CR - MIN, N * CR, PARTS[7:8])]
 
-    def product(k, a, b):
+    def product(k):
+        a, b, _ = BANKS[k]
         t.matmul_mx(T.ps[:, 512 * k:512 * k + b - a], T.qw[:, 0:128], T.sw[:, 0:128], T.qb[:, a:b], T.sb[:, a:b],
                     True, True).then_inc(S["t_%d" % k], 1)
     t.wait_ge(S.v_qw, 1)
+    t.wait_ge(S.r_oq, n_in(False))
+    t.wait_ge(S.r_s, n_in(False))
+    product(0)
     t.wait_ge(S.v_b, 2)
     t.wait_ge(S.a_b, 2)
-    t.wait_ge(S.r_oq, n_in(True))
-    t.wait_ge(S.r_os, n_in(False))
-    product(0, 0, 4 * CR)
-    product(1, 5 * CR - MIN, 5 * CR)
-    for j, m in enumerate(mates):
-        t.wait_ge(S["r_gq%d" % j], n_from(m, True))
-        t.wait_ge(S["r_gs%d" % j], n_from(m, False))
-        product(2 + j, (6 + j) * CR - MIN, (6 + j) * CR)
+    product(1)
+    for k in (2, 3, 4):
+        j = BANKS[k][2][0][0]
+        t.wait_ge(S["r_gq%d" % j], n_from(mates[j], True))
+        product(k)
 
-    def new(k):
-        return T.ps[:, 512 * k + MIN - CR:512 * k + MIN]
-
-    def res_of(c):
-        q = rank_of[c]
-        return T.res[:, q * CR:(q + 1) * CR]
-    lo = rank_of[mine[0]] * CR
-    A.wait_ge(S.t_0, 1)
-    A.activation(T.res[:, lo:lo + 4 * CR], T.ps[:, 0:4 * CR], COPY).then_inc(S.a_c, 1)
-    A.wait_ge(S.t_4, 1)
-    A.activation(res_of(partner(mates[2])), new(4), COPY).then_inc(S.a_c, 1)
-    for k, c in ((1, par), (2, partner(mates[0])), (3, partner(mates[1]))):
-        V.wait_ge(S["t_%d" % k], 1)
-        V.tensor_copy(res_of(c), new(k)).then_inc(S.v_c, 1)
+    def empty(q, k):
+        q.wait_ge(S["t_%d" % k], 1)
+        for j, far in BANKS[k][2]:
+            c = core if j is None else mates[j]
+            r = rank_of[partner(c) if far else c]
+            a = 512 * k + at(j, far) - BANKS[k][0]
+            if q is V:
+                V.tensor_copy(T.res[:, r * CR:(r + 1) * CR], T.ps[:, a:a + CR]).then_inc(S.v_c, 1)
+            else:
+                A.activation(T.res[:, r * CR:(r + 1) * CR], T.ps[:, a:a + CR], COPY).then_inc(S.a_c, 1)
+    for q, ks in ((A, (0, 2, 3)), (V, (1, 4))):
+        for k in ks:
+            empty(q, k)
     for q in (V, A):
-        q.wait_ge(S.v_po, 1)
-        q.wait_ge(S.v_c, 3)
-        q.wait_ge(S.a_c, 2)
-    V.tensor_copy(T.yt[:, 0:W // 2], T.res[:, :].indirect(T.poff[:, 0:16])).then_inc(S.v_y, 1)
-    A.activation(T.yt[:, W // 2:W], T.res[:, :].indirect(T.poff[:, 16:32]), COPY).then_inc(S.a_y, 1)
-    g.sync.wait_ge(S.v_y, 1)
-    g.sync.wait_ge(S.a_y, 1)
-    g.sync.dma_start(T.y[:, :], T.yt[:, :]).then_inc(S.d_y, 16)
-    g.sync.wait_ge(S.d_y, 16)
+        q.wait_ge(S.a_c, 4)
+        q.wait_ge(S.v_c, 4)
+
+    def cut(half, k):
+        return half * W // 2 + YCUTS[k], half * W // 2 + YCUTS[k + 1]
+
+    def piece(half, k):
+        a, b = cut(half, k)
+        return T.yt[:, a:b], T.res[:, :].indirect(T.loff[:, P0 + a // 16:P0 + b // 16])
+    last = len(YCUTS) - 2
+    for k in range(last + 1):
+        V.tensor_copy(*piece(0, k)).then_inc(S.v_y, 1)
+        A.activation(*piece(1, k), COPY).then_inc(S.a_y, 1)
+        for half, sem in enumerate((S.v_y, S.a_y)):
+            queue = A if (half, k) == (1, last) else g.sync
+            a, b = cut(half, k)
+            queue.wait_ge(sem, k + 1)
+            queue.dma_start(T.y[:, a:b], T.yt[:, a:b]).then_inc(S.d_y, 16)
+    g.sync.wait_ge(S.d_y, 32 * (last + 1))
 
     def span(m):
         a = min(rank_of[m], rank_of[partner(m)]) * CC
-        return T.noff[:, a:a + LW]
+        return T.loff[:, a:a + LW]
 
     def q8(t, a, n):
         return t[:, a:a + n].bitcast(dt.uint8)
 
     def s8(t, a, n):
         return t[:, a:a + n]
-    g.wait_ge(S.v_no, 1)
+    g.wait_ge(S.v_lo, 4)
     to_mates((0, 1, 2), lambda j: span(mates[j]), lambda m: T.nland[:, place(m, core) * LW:(place(m, core) + 1) * LW],
              lambda m: S.r_list, False)
     rid, pid = topo.addr(par, core)
-    for picked, view, dst, src, arrived in ((S.v_ru, q8, T.qgu, T.qru, S.r_uq), (S.a_ru, s8, T.sgu, T.sru, S.r_us)):
-        g.wait_ge(picked, 1)
-        g.remote_dma(out_ap=view(dst, 0, UN), in_ap=view(src, 0, UN), remote_sem=arrived, local_sem=S.ls, pid=pid,
+    for picked, n, view, dst, src, a, b, arrived in ((S.v_ru, 1, q8, T.qgu, T.qru, 0, U1, S.r_uq),
+                                                     (S.a_ru, 2, s8, T.sgu, T.sru, 0, UN, S.r_us),
+                                                     (S.v_ru, 2, q8, T.qgu, T.qru, U1, UN, S.r_uq)):
+        g.wait_ge(picked, n)
+        g.remote_dma(out_ap=view(dst, a, b - a), in_ap=view(src, a, b - a), remote_sem=arrived, local_sem=S.ls, pid=pid,
                      routing_id=rid, dma_engine_mask=bits(par_eng))
-    for k, js in ((1, (2,)), (3, (1, 0))):
-        g.wait_ge(S.v_op, k)
-        to_mates(js, lambda j: q8(T.qop, OP[j], CR), lambda m: q8(T.qb, slot * CR, CR), lambda m: S.r_oq, True)
-    g.wait_ge(S.a_op, 3)
-    to_mates((0, 1, 2), lambda j: s8(T.sop, OP[j], CR), lambda m: s8(T.sb, slot * CR, CR), lambda m: S.r_os, False)
-
-    def at(m):
-        return (5 + place(m, core)) * CR
-    for k, js in ((1, (1,)), (3, (0, 2))):
-        g.wait_ge(S.v_gp, k)
-        to_mates(js, lambda j: q8(T.qgp, GP[j], CR), lambda m: q8(T.qb, at(m), CR),
+    g.wait_ge(S.v_op, 3)
+    to_mates((0, 1, 2), lambda j: q8(T.qp, out_at(j, False), CR), lambda m: q8(T.qb, at(place(m, core), False), CR),
+             lambda m: S.r_oq, False)
+    g.wait_ge(S.a_p, 6)
+    to_mates((0, 1, 2), lambda j: s8(T.sp, 2 * j * CR, 2 * CR), lambda m: s8(T.sb, pair(place(m, core)), 2 * CR),
+             lambda m: S.r_s, False)
+    for k, j in enumerate(GP):
+        g.wait_ge(S.v_gp, k + 1)
+        to_mates((j,), lambda j: q8(T.qp, out_at(j, True), CR), lambda m: q8(T.qb, at(place(m, core), True), CR),
                  lambda m: S["r_gq%d" % place(m, core)], True)
-    g.wait_ge(S.a_gp, 3)
-    to_mates((0, 1, 2), lambda j: s8(T.sgp, GP[j], CR), lambda m: s8(T.sb, at(m), CR),
-             lambda m: S["r_gs%d" % place(m, core)], False)
-    g.wait_ge(S.ls, 2 * len(par_eng) + sum(sent))
+    g.wait_ge(S.ls, 3 * len(par_eng) + sum(sent))

from concourse.bass import DstId, RemoteDMATransfer
from concourse.mybir import dt, ActivationFunctionType

TC, W, UN, CR = 1024, 512, 224, 96
N = 8
UC, CC = UN // 16, CR // 16
CUTS = (0, 192, 640, 896, TC)
U1 = 64
LW = (N // 2 + 1) * CC
U0, P0 = N * CC, N * CC + 2 * UC
NU = P0 + W // 16
MIN = 128
YCUTS = (0, 64, 160, W // 2)
CODES, PLANE = "float8_e4m3fn_x4", "uint8"

SCRATCH = {
    "lsti": ("sbuf", [128, NU], "int32"),
    "loff": ("sbuf", [128, NU], "uint16"),
    "nland": ("sbuf", [128, 3 * LW], "uint16"),
    "ct": ("sbuf", [128, 4 * TC], "bfloat16"),
    "wt": ("sbuf", [128, 512], "bfloat16"),
    "qc": ("sbuf", [128, TC], CODES), "sc": ("sbuf", [128, TC], PLANE),
    "qw": ("sbuf", [128, 128], CODES), "sw": ("sbuf", [128, 128], PLANE),
    "qru": ("sbuf", [128, UN], CODES), "sru": ("sbuf", [128, UN], PLANE),
    "qou": ("sbuf", [128, UN], CODES), "sou": ("sbuf", [128, UN], PLANE),
    "qgu": ("sbuf", [128, UN], CODES), "sgu": ("sbuf", [128, UN], PLANE),
    "qp": ("sbuf", [128, 6 * CR], CODES), "sp": ("sbuf", [128, 6 * CR], PLANE),
    "qb": ("sbuf", [128, N * CR], CODES), "sb": ("sbuf", [128, N * CR], PLANE),
    "res": ("sbuf", [128, N * CR], "float32"),
    "yt": ("sbuf", [128, W], "float32"),
    "ps": ("psum", [128, 5 * 512], "float32"),
}
SEMAPHORES = ["d_lst", "d_c0", "d_c1", "d_c2", "d_c3", "d_w", "d_y",
              "v_lo", "v_q", "v_qw", "v_ru", "v_ou", "v_op", "v_gp", "v_b", "v_c", "v_y",
              "a_ru", "a_ou", "a_p", "a_b", "a_c", "a_y",
              "t_0", "t_1", "t_2", "t_3", "t_4",
              "r_list", "r_uq", "r_us", "r_oq", "r_s",
              "r_gq0", "r_gq1", "r_gq2", "ls"]


def rank_program(g, core, T, topo):
    if T.rank_of(core) is None:
        return
    S = T.sem
    COPY = ActivationFunctionType.Copy
    cores = list(T.cores)
    rank_of = {c: r for r, c in enumerate(cores)}

    def home(c):
        return [d for d in cores if topo.host(d) == topo.host(c)]

    def mates_of(c):
        on = topo.cores_of(c)
        m = [d for d in home(c) if d != c]
        off = [d for d in m if d not in on]
        return ([d for d in m if d in on] + [d for d in off if topo.die(d) != topo.die(c)]
                + [d for d in off if topo.die(d) == topo.die(c)])

    def place(m, c):
        return mates_of(m).index(c)

    def partner(c):
        return [d for d in cores if topo.host(d) != topo.host(c) and topo.same_plane(c, d) and topo.die(d) == topo.die(c)][0]

    mates = mates_of(core)
    par = partner(core)
    h = topo.host(core) - topo.host(cores[0])
    oh = 1 - h

    def bits(es):
        return sum(1 << e for e in es)

    def engines(c, m, whole):
        ms = mates_of(c)
        leave = topo.engines(c, ms[1])
        if m == ms[0]:
            return [e for e in topo.engines(c, m) if e not in leave]
        if whole:
            return leave
        n = len(leave) // 2
        return leave[:n] if m == ms[1] else leave[n:]

    sent = []

    def to_mates(js, src, dst, sem, whole):
        tr = []
        for j in js:
            m = mates[j]
            rid, pid = topo.addr(m, core)
            es = engines(core, m, whole)
            sent.append(len(es))
            tr.append(RemoteDMATransfer(dst_ids=[DstId(rid=rid, pnc=pid)], dma_engine_mask=bits(es), remote_sem=sem(m),
                                        src=src(j), dst=dst(m)))
        g.remote_dma_fused(tr, local_sem=S.ls)

    def n_from(m, whole):
        return len(engines(m, core, whole))

    def n_in(whole):
        return sum(n_from(m, whole) for m in mates)
    par_eng = topo.engines(core, par)
    n_par_in = len(topo.engines(par, core))

    V, A = g.vector, g.scalar

    def load_c(k):
        a, b = CUTS[k], CUTS[k + 1]
        g.sync.dma_start(T.ct[:, 4 * a:4 * b], T.c[:, 4 * a:4 * b]).then_inc(S["d_c%d" % k], 16)
    load_c(0)
    for k, queue in enumerate((g.sync, A)):
        for a, b, lst in ((0, U0, T.need), (U0, P0, T.uni), (P0, NU, T.pos)):
            queue.dma_start(T.lsti[16 * k:16 * k + 16, a:b], lst[:, :]).then_inc(S.d_lst, 16)
    for k in range(1, 4):
        load_c(k)
    g.sync.dma_start(T.wt[:, :], T.w[:, :]).then_inc(S.d_w, 16)

    V.wait_ge(S.d_lst, 96)
    for k in range(4):
        V.tensor_copy(T.loff[32 * k:32 * k + 32, :], T.lsti[0:32, :]).then_inc(S.v_lo, 1)
    for k in range(4):
        a, b = CUTS[k], CUTS[k + 1]
        V.wait_ge(S["d_c%d" % k], 16)
        V.quantize_mx(T.qc[:, a:b], T.sc[:, a:b], T.ct[:, 4 * a:4 * b]).then_inc(S.v_q, 1)

    def pick_q(out, a, n, win, offs, sem):
        V.tensor_copy(out[:, a:a + n].bitcast(dt.uint32), win[:, :].bitcast(dt.uint32).indirect(offs)).then_inc(sem, 1)

    def pick_s(out, a, n, win, offs, sem):
        A.activation(out[:, a:a + n], win[:, :].indirect(offs), COPY).then_inc(sem, 1)

    def wanted(j, c):
        a = j * LW + (rank_of[c] - min(rank_of[core], rank_of[par])) * CC
        return T.nland[:, a:a + CC]

    def own_need(c):
        return T.loff[:, rank_of[c] * CC:(rank_of[c] + 1) * CC]

    def uni(hh, a, b):
        return T.loff[:, U0 + hh * UC + a // 16:U0 + hh * UC + b // 16]
    GP = (1, 0, 2)
    PARTS = [(None, True), (None, False), (1, False), (1, True), (0, True), (0, False), (2, False), (2, True)]

    def at(j, far):
        return PARTS.index((j, far)) * CR

    def pair(j):
        return min(at(j, False), at(j, True))

    def out_at(j, far):
        return 2 * j * CR + at(j, far) - pair(j)

    for q, pick, far, near, win, out, s_ru, s_ou, s_op in (
            (V, pick_q, T.qru, T.qou, T.qc, T.qp, S.v_ru, S.v_ou, S.v_op),
            (A, pick_s, T.sru, T.sou, T.sc, T.sp, S.a_ru, S.a_ou, S.a_p)):
        q.wait_ge(S.v_lo, 4)
        q.wait_ge(S.v_q, 4)
        for a, b in ((0, U1), (U1, UN)):
            pick(far, a, b - a, win, uni(oh, a, b), s_ru)
        pick(near, 0, UN, win, uni(h, 0, UN), s_ou)
        q.wait_ge(s_ou, 1)
        q.wait_ge(S.r_list, n_in(False))
        for j in range(3):
            pick(out, out_at(j, False), CR, near, wanted(j, core), s_op)
    pick_q(T.qb, at(None, False), CR, T.qou, own_need(core), S.v_b)
    V.wait_ge(S.d_w, 16)
    V.quantize_mx(T.qw[:, 0:128], T.sw[:, 0:128], T.wt[:, 0:512]).then_inc(S.v_qw, 1)
    V.wait_ge(S.r_uq, 2 * n_par_in)
    for j in GP:
        pick_q(T.qp, out_at(j, True), CR, T.qgu, wanted(j, par), S.v_gp)
    pick_q(T.qb, at(None, True), CR, T.qgu, own_need(par), S.v_b)
    A.wait_ge(S.r_us, n_par_in)
    for j in GP:
        pick_s(T.sp, out_at(j, True), CR, T.sgu, wanted(j, par), S.a_p)
    pick_s(T.sb, at(None, False), CR, T.sou, own_need(core), S.a_b)
    pick_s(T.sb, at(None, True), CR, T.sgu, own_need(par), S.a_b)

    t = g.tensor
    BANKS = [(at(0, False), at(2, True), PARTS[5:7]), (0, at(1, True), PARTS[0:3]),
             (at(0, True) - MIN, at(0, True), PARTS[3:4]), (at(0, True), at(0, True) + MIN, PARTS[4:5]),
             (N * CR - MIN, N * CR, PARTS[7:8])]

    def product(k):
        a, b, _ = BANKS[k]
        t.matmul_mx(T.ps[:, 512 * k:512 * k + b - a], T.qw[:, 0:128], T.sw[:, 0:128], T.qb[:, a:b], T.sb[:, a:b],
                    True, True).then_inc(S["t_%d" % k], 1)
    t.wait_ge(S.v_qw, 1)
    t.wait_ge(S.r_oq, n_in(False))
    t.wait_ge(S.r_s, n_in(False))
    product(0)
    t.wait_ge(S.v_b, 2)
    t.wait_ge(S.a_b, 2)
    product(1)
    for k in (2, 3, 4):
        j = BANKS[k][2][0][0]
        t.wait_ge(S["r_gq%d" % j], n_from(mates[j], True))
        product(k)

    def empty(q, k):
        q.wait_ge(S["t_%d" % k], 1)
        for j, far in BANKS[k][2]:
            c = core if j is None else mates[j]
            r = rank_of[partner(c) if far else c]
            a = 512 * k + at(j, far) - BANKS[k][0]
            if q is V:
                V.tensor_copy(T.res[:, r * CR:(r + 1) * CR], T.ps[:, a:a + CR]).then_inc(S.v_c, 1)
            else:
                A.activation(T.res[:, r * CR:(r + 1) * CR], T.ps[:, a:a + CR], COPY).then_inc(S.a_c, 1)
    for q, ks in ((A, (0, 2, 3)), (V, (1, 4))):
        for k in ks:
            empty(q, k)
    for q in (V, A):
        q.wait_ge(S.a_c, 4)
        q.wait_ge(S.v_c, 4)

    def cut(half, k):
        return half * W // 2 + YCUTS[k], half * W // 2 + YCUTS[k + 1]

    def piece(half, k):
        a, b = cut(half, k)
        return T.yt[:, a:b], T.res[:, :].indirect(T.loff[:, P0 + a // 16:P0 + b // 16])
    last = len(YCUTS) - 2
    for k in range(last + 1):
        V.tensor_copy(*piece(0, k)).then_inc(S.v_y, 1)
        A.activation(*piece(1, k), COPY).then_inc(S.a_y, 1)
        for half, sem in enumerate((S.v_y, S.a_y)):
            queue = A if (half, k) == (1, last) else g.sync
            a, b = cut(half, k)
            queue.wait_ge(sem, k + 1)
            queue.dma_start(T.y[:, a:b], T.yt[:, a:b]).then_inc(S.d_y, 16)
    g.sync.wait_ge(S.d_y, 32 * (last + 1))

    def span(m):
        a = min(rank_of[m], rank_of[partner(m)]) * CC
        return T.loff[:, a:a + LW]

    def q8(t, a, n):
        return t[:, a:a + n].bitcast(dt.uint8)

    def s8(t, a, n):
        return t[:, a:a + n]
    g.wait_ge(S.v_lo, 4)
    to_mates((0, 1, 2), lambda j: span(mates[j]), lambda m: T.nland[:, place(m, core) * LW:(place(m, core) + 1) * LW],
             lambda m: S.r_list, False)
    rid, pid = topo.addr(par, core)
    for picked, n, view, dst, src, a, b, arrived in ((S.v_ru, 1, q8, T.qgu, T.qru, 0, U1, S.r_uq),
                                                     (S.a_ru, 2, s8, T.sgu, T.sru, 0, UN, S.r_us),
                                                     (S.v_ru, 2, q8, T.qgu, T.qru, U1, UN, S.r_uq)):
        g.wait_ge(picked, n)
        g.remote_dma(out_ap=view(dst, a, b - a), in_ap=view(src, a, b - a), remote_sem=arrived, local_sem=S.ls, pid=pid,
                     routing_id=rid, dma_engine_mask=bits(par_eng))
    g.wait_ge(S.v_op, 3)
    to_mates((0, 1, 2), lambda j: q8(T.qp, out_at(j, False), CR), lambda m: q8(T.qb, at(place(m, core), False), CR),
             lambda m: S.r_oq, False)
    g.wait_ge(S.a_p, 6)
    to_mates((0, 1, 2), lambda j: s8(T.sp, 2 * j * CR, 2 * CR), lambda m: s8(T.sb, pair(place(m, core)), 2 * CR),
             lambda m: S.r_s, False)
    for k, j in enumerate(GP):
        g.wait_ge(S.v_gp, k + 1)
        to_mates((j,), lambda j: q8(T.qp, out_at(j, True), CR), lambda m: q8(T.qb, at(place(m, core), True), CR),
                 lambda m: S["r_gq%d" % place(m, core)], True)
    g.wait_ge(S.ls, 3 * len(par_eng) + sum(sent))
